import numpy as np
import ml_dtypes


def mxq(x, axis, fmt="e4m3"):
    dtype, down = {"e4m3": (ml_dtypes.float8_e4m3fn, 7), "e5m2": (ml_dtypes.float8_e5m2, 14)}[fmt]
    v = np.moveaxis(np.asarray(x, np.float32).astype(ml_dtypes.bfloat16).astype(np.float64), axis, -1)
    blocks = v.reshape(v.shape[:-1] + (-1, 32))
    amax = np.abs(blocks).max(-1, keepdims=True)
    byte = np.maximum(np.where(amax > 0, np.frexp(amax)[1] - 1 + 127, 0) - down, 1)
    scale = np.exp2(byte - 127.0)
    codes = (blocks / scale).astype(np.float32).astype(dtype).astype(np.float64)
    return np.moveaxis((codes * scale).reshape(v.shape), -1, axis)


WIDE = False


def mx_kscale(k):
    if not WIDE:
        return np.ones(k)
    levels = np.array([30, -30])
    if k % 512:
        return np.exp2(np.random.permutation(np.resize(levels, k // 32))).repeat(32)
    a = np.empty((k // 512, 16))
    for p in range(k // 512):
        a[p, :8] = np.random.permutation(np.resize(levels, 8))
        for g in range(8):
            far = levels[np.abs(levels - a[p, g]) >= 10]
            a[p, g + 8] = far[np.random.randint(len(far))]
    return np.exp2(a.ravel()).repeat(32)


BF16 = ml_dtypes.bfloat16


def bf(x):
    return np.asarray(x, np.float32).astype(BF16)


def f64(x):
    return np.asarray(x).astype(np.float64)


E2M1 = np.array([0.0, 0.5, 1.0, 1.5, 2.0, 3.0, 4.0, 6.0, -0.0, -0.5, -1.0, -1.5, -2.0, -3.0, -4.0, -6.0])


def pack_weight(w, fmt):
    k, n = w.shape
    w = f64(bf(w)).reshape(k // 32, 32, n)
    amax = np.abs(w).max(1)
    if fmt == "e4m3":
        byte = np.frexp(amax)[1] - 1 + 127 - 7
    else:
        mant, ex = np.frexp(amax / 6.0)
        byte = np.where(mant > 0.5, ex, ex - 1) + 127
    byte = np.clip(np.where(amax > 0, byte, 1), 1, 254)
    scaled = (w * np.exp2(127.0 - byte)[:, None, :]).reshape(k, n).astype(np.float32)
    by_word = np.ascontiguousarray(scaled.reshape(k // 512, 128, 4, n).transpose(0, 1, 3, 2))
    if fmt == "e4m3":
        words = by_word.astype(ml_dtypes.float8_e4m3fn).view(np.uint8)
    else:
        c = by_word.astype(ml_dtypes.float4_e2m1fn).view(np.uint8) & 0xF
        words = c[..., 0::2] | (c[..., 1::2] << 4)
    return np.ascontiguousarray(words), np.ascontiguousarray(byte.astype(np.uint8).reshape(k // 512, 16, n))


def unpack_weight(words, scales, fmt):
    g, p, n, _ = words.shape
    if fmt == "e4m3":
        vals = np.ascontiguousarray(words).view(ml_dtypes.float8_e4m3fn).astype(np.float64)
    else:
        nib = np.empty((g, p, n, 4), np.uint8)
        nib[..., 0::2] = words & 0xF
        nib[..., 1::2] = words >> 4
        vals = E2M1[nib]
    vals = vals * np.repeat(np.exp2(scales.astype(np.float64) - 127.0), 8, axis=1)[..., None]
    return vals.transpose(0, 1, 3, 2).reshape(g * 512, n)
def pack4(w):
    words, scales = pack_weight(w, "e2m1")
    return words.reshape(words.shape[0], 128, -1), scales


def unpack4(words, scales):
    return unpack_weight(words.reshape(words.shape[0], 128, -1, 2), scales, "e2m1")


M, K, N, R, L = 1024, 1024, 2048, 1024, 4
CORE = 1.0


def setup_inputs():
    s, t = mx_kscale(K), mx_kscale(N)
    e = np.random.standard_normal(K) * np.sqrt(L / K)
    zx = np.tile(np.random.standard_normal((M, L)) / np.sqrt(L), (1, K // L))
    zc = np.tile(np.random.standard_normal((N, L)) / np.sqrt(L), (1, K // L))
    px = zx * e + 0.3 * np.random.standard_normal((M, K)) / np.sqrt(K)
    pc = zc * e + 0.3 * np.random.standard_normal((N, K)) / np.sqrt(K)
    c_words, c_scales = pack4(-2.0 * pc.T / s[:, None])
    return {"x": bf(px * s),
            "c_words": c_words, "c_scales": c_scales,
            "xn": bf((px * px).sum(1)),
            "cn": bf((pc * pc).sum(1)),
            "stiff": bf((1 + 0.1 * np.random.standard_normal(N)) * t),
            "w": bf(np.random.standard_normal((N, R)) / np.sqrt(N) / t[:, None])}


def reference(x, c_words, c_scales, xn, cn, stiff, w):
    c = unpack4(c_words, c_scales)
    cross = mxq(f64(x), 1, "e4m3") @ c
    d = np.maximum(cross + f64(xn)[:, None] + f64(cn), CORE)
    u = d * np.log(d) * f64(stiff)
    return mxq(u, 1, "e5m2") @ mxq(f64(w), 0, "e4m3")

@@ -1,0 +1,388 @@
+from contextlib import ExitStack
+
+import concourse.mybir as mybir
+from concourse.masks import make_identity
+
+M, K, N, R = 1024, 1024, 2048, 1024
+FLOPS = 2 * M * K * N + 2 * M * N * R
+
+F32 = mybir.dt.float32
+BF16 = mybir.dt.bfloat16
+I32 = mybir.dt.int32
+U32 = mybir.dt.uint32
+U8 = mybir.dt.uint8
+E4M3 = mybir.dt.float8_e4m3fn_x4
+E5M2 = mybir.dt.float8_e5m2_x4
+E2M1 = mybir.dt.float4_e2m1fn_x4
+ALU = mybir.AluOpType
+ACT = mybir.ActivationFunctionType
+
+P = 128
+BANK = 512
+SLOTS = 4
+K_PASSES = K // 512
+N_PASSES = N // 512
+ROW_TILES = M // P
+HALVES = M // BANK
+TILES_PER_HALF = BANK // P
+R_HALVES = R // BANK
+STEPS = HALVES * N_PASSES
+
+
+def tile_thin_plate_radial_term_s9_kernel(tc, x, c_words, c_scales, xn, cn, stiff, w, out):
+    nc = tc.nc
+    x_rows = x.rearrange("(p j) k -> p j k", j=ROW_TILES)
+    out_rows = out.rearrange("(p j) r -> p j r", j=ROW_TILES)
+    w_sets = w.rearrange("(q c r) f -> c q r f", q=16, c=16, r=8)
+
+    with ExitStack() as ctx:
+        keep = ctx.enter_context(tc.tile_pool(name="keep", bufs=1))
+        ring = ctx.enter_context(tc.tile_pool(name="ring", bufs=2))
+        ps_a = ctx.enter_context(tc.psum_pool(name="ps_a", bufs=4))
+        ps_b = ctx.enter_context(tc.psum_pool(name="ps_b", bufs=4))
+        ctx.enter_context(tc.manual_schedule())
+
+        ident32 = keep.tile([P, P], F32, name="ident32")
+        ident16 = keep.tile([P, P], BF16, name="ident16")
+        vec_rows = keep.tile([P, P], BF16, name="vec_rows")
+        xn_cols = keep.tile([P, ROW_TILES], BF16, name="xn_cols")
+        xn_wide = keep.tile([P, M], BF16, name="xn_wide")
+        vec_cols = keep.tile([P, 32], F32, name="vec_cols")
+        divisor = keep.tile([P, 16], F32, name="divisor")
+        inverse = keep.tile([P, 16], F32, name="inverse")
+        neg_stiff = keep.tile([P, 16], F32, name="neg_stiff")
+        residual = keep.tile([P, 16], F32, name="residual")
+        c_raw = keep.tile([P, K_PASSES, 2 * N], U8, name="c_raw")
+        cs_raw = keep.tile([P, K_PASSES, N], U8, name="cs_raw")
+        x_raw = [keep.tile([P, K], BF16, name="x_raw%d" % j) for j in range(ROW_TILES)]
+        w_raw = [keep.tile([P, SLOTS, R], BF16, name="w_raw%d" % g) for g in range(N_PASSES)]
+        c_codes = [keep.tile([P, K_PASSES, 2 * BANK], U8, name="c_codes%d" % g, align_bytes=64) for g in range(N_PASSES)]
+        c_scale = [keep.tile([P, K_PASSES, BANK], U8, name="c_scale%d" % g, align_bytes=64) for g in range(N_PASSES)]
+        x_codes = [keep.tile([P, K_PASSES, BANK], U32, name="x_codes%d" % h, align_bytes=64) for h in range(HALVES)]
+        x_scale = [keep.tile([P, K_PASSES, BANK], U8, name="x_scale%d" % h, align_bytes=64) for h in range(HALVES)]
+        w_codes = {}
+        w_scale = {}
+        for g in range(N_PASSES):
+            for rh in range(R_HALVES):
+                w_codes[g, rh] = keep.tile([P, BANK], U32, name="w_codes%d_%d" % (g, rh), align_bytes=64)
+                w_scale[g, rh] = keep.tile([P, BANK], U8, name="w_scale%d_%d" % (g, rh), align_bytes=64)
+
+        nc.vector.memset(vec_rows[:], 0.0)
+        nc.vector.memset(cs_raw[:].rearrange("p a n -> p (a n)").bitcast(I32), 0)
+        make_identity(nc, ident16[:])
+        make_identity(nc, ident32[:])
+
+        def load_x(j):
+            nc.sync.dma_start(out=x_raw[j][:], in_=x_rows[:, j, :])
+
+        def load_w(g):
+            for t in range(SLOTS):
+                nc.sync.dma_start(out=w_raw[g][:, t, :], in_=w_sets[SLOTS * g + t])
+
+        nc.sync.dma_start(out=xn_cols[:], in_=xn.rearrange("(p j) -> p j", j=ROW_TILES))
+        load_x(0)
+        for row0, vec in ((0, cn), (16, stiff)):
+            nc.sync.dma_start(
+                out=vec_rows[row0 : row0 + 16, :].rearrange("c (q r) -> c q r", r=8),
+                in_=vec.rearrange("(q c r) -> c q r", q=16, c=16, r=8),
+            )
+        for j in (1, 2, 3):
+            load_x(j)
+        for quad in range(4):
+            nc.sync.dma_start(
+                out=cs_raw[32 * quad : 32 * quad + 4, :, :].bitcast(I32),
+                in_=c_scales[:, 4 * quad : 4 * quad + 4, :].rearrange("a r n -> r a n").bitcast(I32),
+            )
+        nc.sync.dma_start(out=c_raw[:].bitcast(I32), in_=c_words.rearrange("a p n -> p a n").bitcast(I32))
+        load_w(0)
+        for j in (4, 5, 6, 7):
+            load_x(j)
+        load_w(1)
+        load_w(2)
+        load_w(3)
+
+        x_banks = {}
+        x_pairs = {}
+
+        x_sorted = {}
+
+        def sort_x(j):
+            x_sorted[j] = ring.tile([P, K // 2], F32, name="x_sorted", bufs=4)
+            nc.vector.tensor_copy(
+                out=x_sorted[j][:].rearrange("p (a u w) -> p a u w", a=K_PASSES, u=2),
+                in_=x_raw[j][:].bitcast(F32).rearrange("p (a w u) -> p a u w", a=K_PASSES, u=2),
+            )
+
+        def turn_x(j):
+            bank = ps_b.tile([P, BANK], F32, name="bank_b")
+            words = x_raw[j][:].bitcast(F32)
+            for kp in range(K_PASSES):
+                for u in range(2):
+                    col0 = (2 * kp + u) * P
+                    if j in x_sorted:
+                        block = x_sorted[j][:, col0 : col0 + P]
+                    else:
+                        block = words[:, 256 * kp + u : 256 * (kp + 1) : 2]
+                    nc.tensor.transpose(bank[:, col0 : col0 + P], block, ident32[:])
+            x_banks[j] = bank
+
+        def spill_x(j, on_vector):
+            if j % 2 == 0:
+                x_pairs[j // 2] = ring.tile([P, K_PASSES, 2 * P, 2], F32, name="x_pair", align_bytes=64)
+            dst = x_pairs[j // 2][:, :, (j % 2) * P : (j % 2 + 1) * P, :]
+            src = x_banks[j][:].rearrange("p (a u m) -> p a m u", a=K_PASSES, u=2)
+            if on_vector:
+                nc.vector.tensor_copy(out=dst, in_=src)
+            else:
+                nc.scalar.copy(out=dst, in_=src)
+
+        def quantise_x(a):
+            h, col0 = a // 2, (a % 2) * 2 * P
+            for kp in range(K_PASSES):
+                nc.vector.quantize_mx(
+                    out=x_codes[h][:, kp, col0 : col0 + 2 * P].bitcast(E4M3),
+                    scales=x_scale[h][:, kp, col0 : col0 + 2 * P],
+                    in_=x_pairs[a][:, kp, :, :].rearrange("p m u -> p (m u)").bitcast(BF16),
+                )
+
+        def deal_c(g):
+            src = c_raw[:].bitcast(I32).rearrange("p a (q c e) -> p a c q e", q=16, c=16)
+            nc.vector.tensor_copy(
+                out=c_codes[g][:].bitcast(I32).rearrange("p a (c q e) -> p a c q e", c=SLOTS, q=16),
+                in_=src[:, :, SLOTS * g : SLOTS * (g + 1), :, :],
+            )
+
+        def deal_cs(g):
+            src = cs_raw[:].bitcast(I32).rearrange("p a (q c e) -> p a c q e", q=16, c=16)
+            nc.vector.tensor_copy(
+                out=c_scale[g][:].bitcast(I32).rearrange("p a (c q e) -> p a c q e", c=SLOTS, q=16),
+                in_=src[:, :, SLOTS * g : SLOTS * (g + 1), :, :],
+            )
+
+        w_mixed = {}
+
+        def mix_w(g, rh):
+            mixed = ring.tile([P, BANK, SLOTS], BF16, name="w_mixed", bufs=4, align_bytes=64)
+            nc.scalar.copy(
+                out=mixed[:].rearrange("p (c i) t -> p c t i", i=4),
+                in_=w_raw[g][:, :, rh * BANK : (rh + 1) * BANK].rearrange("p t (c i) -> p c t i", i=4),
+            )
+            w_mixed[g, rh] = mixed
+
+        def quantise_w(g, rh):
+            nc.vector.quantize_mx(
+                out=w_codes[g, rh][:].bitcast(E4M3),
+                scales=w_scale[g, rh][:],
+                in_=w_mixed[g, rh][:].rearrange("p f t -> p (f t)"),
+            )
+
+        cross = {}
+
+        def cross_mm(step, t):
+            h, g = divmod(step, N_PASSES)
+            bank = ps_a.tile([P, BANK], F32, name="bank_a")
+            for kp in range(K_PASSES):
+                nc.tensor.matmul_mx(
+                    out=bank[:],
+                    lhsT=c_codes[g][:, kp, 2 * P * t : 2 * P * (t + 1)].bitcast(E2M1),
+                    lhsT_scale=c_scale[g][:, kp, P * t : P * (t + 1)],
+                    rhs=x_codes[h][:, kp, :].bitcast(E4M3),
+                    rhs_scale=x_scale[h][:, kp, :],
+                    start=(kp == 0),
+                    stop=(kp == K_PASSES - 1),
+                )
+            cross[step, t] = bank
+
+        scaled = {}
+        logs = {}
+
+        def add_norms(step, t):
+            h, g = divmod(step, N_PASSES)
+            if t == 0:
+                scaled[step] = ring.tile([P, SLOTS, BANK], F32, name="scaled", bufs=3)
+            c = SLOTS * g + t
+            nc.vector.scalar_tensor_tensor(
+                out=scaled[step][:, t, :],
+                in0=cross[step, t][:],
+                scalar=vec_cols[:, c : c + 1],
+                in1=xn_wide[:, h * BANK : (h + 1) * BANK],
+                op0=ALU.add,
+                op1=ALU.add,
+            )
+
+        def clamp_scale(step, t):
+            c = SLOTS * (step % N_PASSES) + t
+            nc.vector.tensor_scalar(
+                out=scaled[step][:, t, :],
+                in0=scaled[step][:, t, :],
+                scalar1=1.0,
+                scalar2=vec_cols[:, 16 + c : 17 + c],
+                op0=ALU.max,
+                op1=ALU.mult,
+            )
+
+        def take_log(step, t):
+            c = SLOTS * (step % N_PASSES) + t
+            if t == 0:
+                logs[step] = ring.tile([P, SLOTS, BANK], F32, name="logs")
+            nc.scalar.activation(
+                out=logs[step][:, t, :],
+                in_=scaled[step][:, t, :],
+                func=ACT.Ln,
+                scale=inverse[:, c : c + 1],
+                bias=residual[:, c : c + 1],
+            )
+
+        u_mixed = {}
+        u_codes = {}
+        u_scale = {}
+
+        def multiply(step, col0, width):
+            mixed = ring.tile([P, width, SLOTS], BF16, name="u_mixed%d" % width, bufs=(2 if width == BANK else 4), align_bytes=64)
+            cols = slice(col0, col0 + width)
+            nc.vector.tensor_tensor(
+                out=mixed[:].rearrange("p (c i) t -> p c t i", i=2),
+                in0=scaled[step][:, :, cols].rearrange("p t (c i) -> p c t i", i=2),
+                in1=logs[step][:, :, cols].rearrange("p t (c i) -> p c t i", i=2),
+                op=ALU.mult,
+            )
+            u_mixed[step, col0] = mixed
+
+        def quantise_u(step, col0, width):
+            codes = keep.tile([P, width], U32, name="u_codes%d_%d" % (step, col0), align_bytes=64)
+            scales = keep.tile([P, width], U8, name="u_scale%d_%d" % (step, col0), align_bytes=64)
+            nc.vector.quantize_mx(
+                out=codes[:].bitcast(E5M2),
+                scales=scales[:],
+                in_=u_mixed[step, col0][:].rearrange("p m t -> p (m t)"),
+            )
+            for j in range(width // P):
+                u_codes[step, col0 // P + j] = codes[:, j * P : (j + 1) * P]
+                u_scale[step, col0 // P + j] = scales[:, j * P : (j + 1) * P]
+
+        sums = {}
+
+        def out_mm(h, j, rh, g, pool):
+            if g == 0:
+                sums[h, j, rh] = pool.tile([P, BANK], F32, name="bank_a" if pool is ps_a else "bank_b")
+            nc.tensor.matmul_mx(
+                out=sums[h, j, rh][:],
+                lhsT=u_codes[N_PASSES * h + g, j].bitcast(E5M2),
+                lhsT_scale=u_scale[N_PASSES * h + g, j],
+                rhs=w_codes[g, rh][:].bitcast(E4M3),
+                rhs_scale=w_scale[g, rh][:],
+                start=(g == 0),
+                stop=(g == N_PASSES - 1),
+            )
+
+        def out_passes(h, rh, passes, pool):
+            for j in range(TILES_PER_HALF):
+                for g in passes:
+                    out_mm(h, j, rh, g, pool)
+
+        def store(h, j, rh, on_vector):
+            result = ring.tile([P, BANK], F32, name="result", bufs=6)
+            if on_vector:
+                nc.vector.tensor_copy(out=result[:], in_=sums[h, j, rh][:])
+            else:
+                nc.scalar.copy(out=result[:], in_=sums[h, j, rh][:])
+            nc.sync.dma_start(out=out_rows[:, TILES_PER_HALF * h + j, rh * BANK : (rh + 1) * BANK], in_=result[:])
+
+        xn_bank = ps_a.tile([P, M], BF16, name="bank_a")
+        for j in range(ROW_TILES):
+            nc.tensor.transpose(xn_bank[:, j * P : (j + 1) * P], xn_cols[:, j : j + 1].to_broadcast([P, P]), ident16[:])
+        vec_bank = ps_a.tile([P, P], BF16, name="bank_a")
+        nc.tensor.transpose(vec_bank[:], vec_rows[:], ident16[:])
+        for j in range(TILES_PER_HALF):
+            sort_x(j)
+            turn_x(j)
+            if j == 0:
+                nc.scalar.copy(out=xn_wide[:], in_=xn_bank[:])
+            if j == 1:
+                nc.vector.tensor_copy(out=vec_cols[:], in_=vec_bank[:, 0:32])
+            spill_x(j, False)
+        stiff_cols = vec_cols[:, 16:32]
+        nc.vector.scalar_tensor_tensor(out=divisor[:], in0=stiff_cols, scalar=0.0, in1=stiff_cols, op0=ALU.is_equal, op1=ALU.add)
+        nc.vector.tensor_scalar(out=neg_stiff[:], in0=stiff_cols, scalar1=-1.0, scalar2=None, op0=ALU.mult)
+        quantise_x(0)
+        nc.vector.reciprocal(out=inverse[:], in_=divisor[:])
+        deal_cs(0)
+        quantise_x(1)
+        deal_c(0)
+        for c in range(16):
+            nc.scalar.activation(
+                out=residual[:, c : c + 1], in_=neg_stiff[:, c : c + 1], func=ACT.Identity, scale=inverse[:, c : c + 1], bias=1.0
+            )
+        for t in range(SLOTS):
+            cross_mm(0, t)
+        for g in range(1, N_PASSES):
+            deal_cs(g)
+            deal_c(g)
+
+        w_order = [(g, rh) for rh in range(R_HALVES) for g in range(N_PASSES)]
+        mixes = {-1: w_order[0:1], 0: w_order[1:2], 1: w_order[2:3], 2: w_order[3:5], 3: w_order[5:7], 4: w_order[7:8]}
+        for key in mixes[-1]:
+            mix_w(*key)
+
+        for step in range(STEPS):
+            for t in range(SLOTS):
+                add_norms(step, t)
+                if step + 1 < STEPS:
+                    cross_mm(step + 1, t)
+                if t == 1:
+                    if step >= 2:
+                        quantise_u(step - 2, 0, BANK)
+                    for key in mixes.get(step - 2, []):
+                        quantise_w(*key)
+                    if step in (5, 6):
+                        out_passes(0, step - 5, [3] if step == 5 else [2, 3], ps_b)
+                        for j in range(TILES_PER_HALF):
+                            store(0, j, step - 5, False)
+            if step in (0, 1):
+                turn_x(4 + 2 * step)
+                turn_x(5 + 2 * step)
+            if step == 3:
+                out_passes(0, 0, [0, 1], ps_b)
+            if step == 4:
+                out_passes(0, 0, [2], ps_b)
+            if step == 5:
+                out_passes(0, 1, [0, 1], ps_b)
+            if step == 6:
+                out_passes(1, 0, [0], ps_b)
+            if step == 7:
+                out_passes(1, 0, [1], ps_b)
+                out_passes(1, 1, [0, 1], ps_a)
+            for t in range(SLOTS):
+                clamp_scale(step, t)
+                take_log(step, t)
+            if step in (1, 2):
+                quantise_x(step + 1)
+            if step in (0, 1):
+                spill_x(4 + 2 * step, False)
+                spill_x(5 + 2 * step, False)
+            for key in mixes.get(step, []):
+                mix_w(*key)
+            if 1 <= step < STEPS - 1:
+                multiply(step - 1, 0, BANK)
+
+        last = STEPS - 1
+
+        def finish(step, j):
+            quantise_u(step, j * P, P)
+            out_mm(1, j, 0, step - N_PASSES, ps_b)
+            out_mm(1, j, 1, step - N_PASSES, ps_a)
+
+        multiply(last - 1, 0, P)
+        multiply(last - 1, P, P)
+        finish(last - 1, 0)
+        for j in range(TILES_PER_HALF):
+            multiply(last, j * P, P)
+            if j + 1 < TILES_PER_HALF:
+                finish(last - 1, j + 1)
+            if j + 2 < TILES_PER_HALF:
+                multiply(last - 1, (j + 2) * P, P)
+            finish(last, j)
+            store(1, j, 0, False)
+            if j + 1 < TILES_PER_HALF:
+                store(1, j, 1, False)
+        store(1, 3, 1, True)

@@ -27,6 +27,7 @@ HALVES = M // BANK
 TILES_PER_HALF = BANK // P
 R_HALVES = R // BANK
 STEPS = HALVES * N_PASSES
+W_PART = 256
 
 
 def tile_thin_plate_radial_term_s9_kernel(tc, x, c_words, c_scales, xn, cn, stiff, w, out):
@@ -161,19 +162,21 @@ def tile_thin_plate_radial_term_s9_kernel(tc, x, c_words, c_scales, xn, cn, stif
 
         w_mixed = {}
 
-        def mix_w(g, rh):
-            mixed = ring.tile([P, BANK, SLOTS], BF16, name="w_mixed", bufs=4, align_bytes=64)
+        def mix_w(g, rh, part):
+            mixed = ring.tile([P, W_PART, SLOTS], BF16, name="w_mixed", bufs=6, align_bytes=64)
+            col0 = rh * BANK + part * W_PART
             nc.scalar.copy(
                 out=mixed[:].rearrange("p (c i) t -> p c t i", i=4),
-                in_=w_raw[g][:, :, rh * BANK : (rh + 1) * BANK].rearrange("p t (c i) -> p c t i", i=4),
+                in_=w_raw[g][:, :, col0 : col0 + W_PART].rearrange("p t (c i) -> p c t i", i=4),
             )
-            w_mixed[g, rh] = mixed
+            w_mixed[g, rh, part] = mixed
 
-        def quantise_w(g, rh):
+        def quantise_w(g, rh, part):
+            cols = slice(part * W_PART, (part + 1) * W_PART)
             nc.vector.quantize_mx(
-                out=w_codes[g, rh][:].bitcast(E4M3),
-                scales=w_scale[g, rh][:],
-                in_=w_mixed[g, rh][:].rearrange("p f t -> p (f t)"),
+                out=w_codes[g, rh][:, cols].bitcast(E4M3),
+                scales=w_scale[g, rh][:, cols],
+                in_=w_mixed[g, rh, part][:].rearrange("p f t -> p (f t)"),
             )
 
         cross = {}
@@ -237,16 +240,18 @@ def tile_thin_plate_radial_term_s9_kernel(tc, x, c_words, c_scales, xn, cn, stif
         u_codes = {}
         u_scale = {}
 
-        def multiply(step, col0, width):
-            mixed = ring.tile([P, width, SLOTS], BF16, name="u_mixed%d" % width, bufs=(2 if width == BANK else 4), align_bytes=64)
-            cols = slice(col0, col0 + width)
-            nc.vector.tensor_tensor(
-                out=mixed[:].rearrange("p (c i) t -> p c t i", i=2),
+        def multiply(step, col0, col1, engine):
+            if step not in u_mixed:
+                u_mixed[step] = ring.tile(
+                    [P, BANK, SLOTS], BF16, name="u_last" if step == STEPS - 1 else "u_mixed", bufs=1, align_bytes=64
+                )
+            cols = slice(col0, col1)
+            engine.tensor_tensor(
+                out=u_mixed[step][:, cols, :].rearrange("p (c i) t -> p c t i", i=2),
                 in0=scaled[step][:, :, cols].rearrange("p t (c i) -> p c t i", i=2),
                 in1=logs[step][:, :, cols].rearrange("p t (c i) -> p c t i", i=2),
                 op=ALU.mult,
             )
-            u_mixed[step, col0] = mixed
 
         def quantise_u(step, col0, width):
             codes = keep.tile([P, width], U32, name="u_codes%d_%d" % (step, col0), align_bytes=64)
@@ -254,7 +259,7 @@ def tile_thin_plate_radial_term_s9_kernel(tc, x, c_words, c_scales, xn, cn, stif
             nc.vector.quantize_mx(
                 out=codes[:].bitcast(E5M2),
                 scales=scales[:],
-                in_=u_mixed[step, col0][:].rearrange("p m t -> p (m t)"),
+                in_=u_mixed[step][:, col0 : col0 + width, :].rearrange("p m t -> p (m t)"),
             )
             for j in range(width // P):
                 u_codes[step, col0 // P + j] = codes[:, j * P : (j + 1) * P]
@@ -319,32 +324,32 @@ def tile_thin_plate_radial_term_s9_kernel(tc, x, c_words, c_scales, xn, cn, stif
             deal_cs(g)
             deal_c(g)
 
-        w_order = [(g, rh) for rh in range(R_HALVES) for g in range(N_PASSES)]
-        mixes = {-1: w_order[0:1], 0: w_order[1:2], 1: w_order[2:3], 2: w_order[3:5], 3: w_order[5:7], 4: w_order[7:8]}
+        w_order = [(g, rh, part) for rh in range(R_HALVES) for g in range(N_PASSES) for part in range(BANK // W_PART)]
+        mixes = {-1: w_order[0:2], 0: w_order[2:5], 1: w_order[5:8], 2: w_order[8:11], 3: w_order[11:14], 4: w_order[14:16]}
         for key in mixes[-1]:
             mix_w(*key)
 
+        last = STEPS - 1
         for step in range(STEPS):
+            share = 256 if step in (1, 2, 7) else 192
+            if step >= 1:
+                multiply(step - 1, 0, share, nc.gpsimd)
+            if step in (5, 6):
+                out_passes(0, step - 5, [3] if step == 5 else [2, 3], ps_b)
+                for j in range(TILES_PER_HALF):
+                    store(0, j, step - 5, False)
             for t in range(SLOTS):
                 add_norms(step, t)
                 if step + 1 < STEPS:
                     cross_mm(step + 1, t)
-                if t == 1:
-                    if step >= 2:
-                        quantise_u(step - 2, 0, BANK)
-                    for key in mixes.get(step - 2, []):
-                        quantise_w(*key)
-                    if step in (5, 6):
-                        out_passes(0, step - 5, [3] if step == 5 else [2, 3], ps_b)
-                        for j in range(TILES_PER_HALF):
-                            store(0, j, step - 5, False)
+            if step in (1, 2):
+                spill_x(2 + 2 * step, True)
+                spill_x(3 + 2 * step, True)
             if step in (0, 1):
                 turn_x(4 + 2 * step)
                 turn_x(5 + 2 * step)
-            if step == 3:
-                out_passes(0, 0, [0, 1], ps_b)
-            if step == 4:
-                out_passes(0, 0, [2], ps_b)
+            if step in (2, 3, 4):
+                out_passes(0, 0, [step - 2], ps_b)
             if step == 5:
                 out_passes(0, 1, [0, 1], ps_b)
             if step == 6:
@@ -353,36 +358,46 @@ def tile_thin_plate_radial_term_s9_kernel(tc, x, c_words, c_scales, xn, cn, stif
                 out_passes(1, 0, [1], ps_b)
                 out_passes(1, 1, [0, 1], ps_a)
             for t in range(SLOTS):
+                if t == SLOTS - 1 and 1 <= step < last:
+                    multiply(step - 1, share, BANK, nc.vector)
                 clamp_scale(step, t)
                 take_log(step, t)
             if step in (1, 2):
                 quantise_x(step + 1)
-            if step in (0, 1):
-                spill_x(4 + 2 * step, False)
-                spill_x(5 + 2 * step, False)
+            for key in mixes.get(step - 1, []):
+                quantise_w(*key)
             for key in mixes.get(step, []):
                 mix_w(*key)
-            if 1 <= step < STEPS - 1:
-                multiply(step - 1, 0, BANK)
-
-        last = STEPS - 1
+            if 1 <= step < last:
+                quantise_u(step - 1, 0, BANK)
 
         def finish(step, j):
             quantise_u(step, j * P, P)
             out_mm(1, j, 0, step - N_PASSES, ps_b)
             out_mm(1, j, 1, step - N_PASSES, ps_a)
 
-        multiply(last - 1, 0, P)
-        multiply(last - 1, P, P)
+        def multiply_tile(step, j):
+            multiply(step, j * P, (j + 1) * P, nc.vector)
+
         finish(last - 1, 0)
-        for j in range(TILES_PER_HALF):
-            multiply(last, j * P, P)
-            if j + 1 < TILES_PER_HALF:
-                finish(last - 1, j + 1)
-            if j + 2 < TILES_PER_HALF:
-                multiply(last - 1, (j + 2) * P, P)
-            finish(last, j)
-            store(1, j, 0, False)
-            if j + 1 < TILES_PER_HALF:
-                store(1, j, 1, False)
+        finish(last - 1, 1)
+        multiply_tile(last - 1, 2)
+        multiply_tile(last, 0)
+        finish(last - 1, 2)
+        finish(last, 0)
+        store(1, 0, 0, False)
+        store(1, 0, 1, False)
+        multiply_tile(last, 1)
+        multiply_tile(last - 1, 3)
+        finish(last, 1)
+        store(1, 1, 0, False)
+        store(1, 1, 1, False)
+        multiply_tile(last, 2)
+        finish(last - 1, 3)
+        finish(last, 2)
+        store(1, 2, 0, False)
+        store(1, 2, 1, False)
+        multiply_tile(last, 3)
+        finish(last, 3)
+        store(1, 3, 0, False)
         store(1, 3, 1, True)

@@ -325,13 +325,13 @@ def tile_thin_plate_radial_term_s9_kernel(tc, x, c_words, c_scales, xn, cn, stif
             deal_c(g)
 
         w_order = [(g, rh, part) for rh in range(R_HALVES) for g in range(N_PASSES) for part in range(BANK // W_PART)]
-        mixes = {-1: w_order[0:2], 0: w_order[2:5], 1: w_order[5:8], 2: w_order[8:11], 3: w_order[11:14], 4: w_order[14:16]}
+        mixes = {-1: w_order[0:2], 0: w_order[2:6], 1: w_order[6:10], 2: w_order[10:13], 3: w_order[13:16]}
         for key in mixes[-1]:
             mix_w(*key)
 
         last = STEPS - 1
         for step in range(STEPS):
-            share = 256 if step in (1, 2, 7) else 192
+            share = 256 if step in (1, 2) else 160
             if step >= 1:
                 multiply(step - 1, 0, share, nc.gpsimd)
             if step in (5, 6):
@@ -342,6 +342,9 @@ def tile_thin_plate_radial_term_s9_kernel(tc, x, c_words, c_scales, xn, cn, stif
                 add_norms(step, t)
                 if step + 1 < STEPS:
                     cross_mm(step + 1, t)
+                if step == 0 and t >= 1:
+                    clamp_scale(step, t - 1)
+                    take_log(step, t - 1)
             if step in (1, 2):
                 spill_x(2 + 2 * step, True)
                 spill_x(3 + 2 * step, True)
@@ -357,7 +360,7 @@ def tile_thin_plate_radial_term_s9_kernel(tc, x, c_words, c_scales, xn, cn, stif
             if step == 7:
                 out_passes(1, 0, [1], ps_b)
                 out_passes(1, 1, [0, 1], ps_a)
-            for t in range(SLOTS):
+            for t in range(SLOTS - 1 if step == 0 else 0, SLOTS):
                 if t == SLOTS - 1 and 1 <= step < last:
                     multiply(step - 1, share, BANK, nc.vector)
                 clamp_scale(step, t)
@@ -379,9 +382,10 @@ def tile_thin_plate_radial_term_s9_kernel(tc, x, c_words, c_scales, xn, cn, stif
         def multiply_tile(step, j):
             multiply(step, j * P, (j + 1) * P, nc.vector)
 
+        multiply(last - 1, 160, 2 * P, nc.vector)
         finish(last - 1, 0)
-        finish(last - 1, 1)
         multiply_tile(last - 1, 2)
+        finish(last - 1, 1)
         multiply_tile(last, 0)
         finish(last - 1, 2)
         finish(last, 0)

@@ -206,9 +206,9 @@ def tile_thin_plate_radial_term_s9_kernel(tc, x, c_words, c_scales, xn, cn, stif
             c = SLOTS * g + t
             nc.vector.scalar_tensor_tensor(
                 out=scaled[step][:, t, :],
-                in0=cross[step, t][:],
+                in0=xn_wide[:, h * BANK : (h + 1) * BANK],
                 scalar=vec_cols[:, c : c + 1],
-                in1=xn_wide[:, h * BANK : (h + 1) * BANK],
+                in1=cross[step, t][:],
                 op0=ALU.add,
                 op1=ALU.add,
             )
@@ -325,13 +325,13 @@ def tile_thin_plate_radial_term_s9_kernel(tc, x, c_words, c_scales, xn, cn, stif
             deal_c(g)
 
         w_order = [(g, rh, part) for rh in range(R_HALVES) for g in range(N_PASSES) for part in range(BANK // W_PART)]
-        mixes = {-1: w_order[0:2], 0: w_order[2:6], 1: w_order[6:10], 2: w_order[10:13], 3: w_order[13:16]}
+        mixes = {-1: w_order[0:2], 0: w_order[2:5], 1: w_order[5:8], 2: w_order[8:12], 3: w_order[12:15], 4: w_order[15:16]}
         for key in mixes[-1]:
             mix_w(*key)
 
         last = STEPS - 1
         for step in range(STEPS):
-            share = 256 if step in (1, 2) else 160
+            share = P
             if step >= 1:
                 multiply(step - 1, 0, share, nc.gpsimd)
             if step in (5, 6):
@@ -345,9 +345,6 @@ def tile_thin_plate_radial_term_s9_kernel(tc, x, c_words, c_scales, xn, cn, stif
                 if step == 0 and t >= 1:
                     clamp_scale(step, t - 1)
                     take_log(step, t - 1)
-            if step in (1, 2):
-                spill_x(2 + 2 * step, True)
-                spill_x(3 + 2 * step, True)
             if step in (0, 1):
                 turn_x(4 + 2 * step)
                 turn_x(5 + 2 * step)
@@ -369,6 +366,9 @@ def tile_thin_plate_radial_term_s9_kernel(tc, x, c_words, c_scales, xn, cn, stif
                 quantise_x(step + 1)
             for key in mixes.get(step - 1, []):
                 quantise_w(*key)
+            if step in (0, 1):
+                spill_x(4 + 2 * step, False)
+                spill_x(5 + 2 * step, False)
             for key in mixes.get(step, []):
                 mix_w(*key)
             if 1 <= step < last:
@@ -382,7 +382,7 @@ def tile_thin_plate_radial_term_s9_kernel(tc, x, c_words, c_scales, xn, cn, stif
         def multiply_tile(step, j):
             multiply(step, j * P, (j + 1) * P, nc.vector)
 
-        multiply(last - 1, 160, 2 * P, nc.vector)
+        multiply_tile(last - 1, 1)
         finish(last - 1, 0)
         multiply_tile(last - 1, 2)
         finish(last - 1, 1)

from contextlib import ExitStack

import concourse.mybir as mybir
from concourse.masks import make_identity

M, K, N, R = 1024, 1024, 2048, 1024
FLOPS = 2 * M * K * N + 2 * M * N * R

F32 = mybir.dt.float32
BF16 = mybir.dt.bfloat16
I32 = mybir.dt.int32
U32 = mybir.dt.uint32
U8 = mybir.dt.uint8
E4M3 = mybir.dt.float8_e4m3fn_x4
E5M2 = mybir.dt.float8_e5m2_x4
E2M1 = mybir.dt.float4_e2m1fn_x4
ALU = mybir.AluOpType
ACT = mybir.ActivationFunctionType

P = 128
BANK = 512
SLOTS = 4
K_PASSES = K // 512
N_PASSES = N // 512
ROW_TILES = M // P
HALVES = M // BANK
TILES_PER_HALF = BANK // P
R_HALVES = R // BANK
STEPS = HALVES * N_PASSES
W_PART = 256


def tile_thin_plate_radial_term_s9_kernel(tc, x, c_words, c_scales, xn, cn, stiff, w, out):
    nc = tc.nc
    x_rows = x.rearrange("(p j) k -> p j k", j=ROW_TILES)
    out_rows = out.rearrange("(p j) r -> p j r", j=ROW_TILES)
    w_sets = w.rearrange("(q c r) f -> c q r f", q=16, c=16, r=8)

    with ExitStack() as ctx:
        keep = ctx.enter_context(tc.tile_pool(name="keep", bufs=1))
        ring = ctx.enter_context(tc.tile_pool(name="ring", bufs=2))
        ps_a = ctx.enter_context(tc.psum_pool(name="ps_a", bufs=4))
        ps_b = ctx.enter_context(tc.psum_pool(name="ps_b", bufs=4))
        ctx.enter_context(tc.manual_schedule())

        ident32 = keep.tile([P, P], F32, name="ident32")
        ident16 = keep.tile([P, P], BF16, name="ident16")
        vec_rows = keep.tile([P, P], BF16, name="vec_rows")
        xn_cols = keep.tile([P, ROW_TILES], BF16, name="xn_cols")
        xn_wide = keep.tile([P, M], BF16, name="xn_wide")
        vec_cols = keep.tile([P, 32], F32, name="vec_cols")
        divisor = keep.tile([P, 16], F32, name="divisor")
        inverse = keep.tile([P, 16], F32, name="inverse")
        neg_stiff = keep.tile([P, 16], F32, name="neg_stiff")
        residual = keep.tile([P, 16], F32, name="residual")
        c_raw = keep.tile([P, K_PASSES, 2 * N], U8, name="c_raw")
        cs_raw = keep.tile([P, K_PASSES, N], U8, name="cs_raw")
        x_raw = [keep.tile([P, K], BF16, name="x_raw%d" % j) for j in range(ROW_TILES)]
        w_raw = [keep.tile([P, SLOTS, R], BF16, name="w_raw%d" % g) for g in range(N_PASSES)]
        c_codes = [keep.tile([P, K_PASSES, 2 * BANK], U8, name="c_codes%d" % g, align_bytes=64) for g in range(N_PASSES)]
        c_scale = [keep.tile([P, K_PASSES, BANK], U8, name="c_scale%d" % g, align_bytes=64) for g in range(N_PASSES)]
        x_codes = [keep.tile([P, K_PASSES, BANK], U32, name="x_codes%d" % h, align_bytes=64) for h in range(HALVES)]
        x_scale = [keep.tile([P, K_PASSES, BANK], U8, name="x_scale%d" % h, align_bytes=64) for h in range(HALVES)]
        w_codes = {}
        w_scale = {}
        for g in range(N_PASSES):
            for rh in range(R_HALVES):
                w_codes[g, rh] = keep.tile([P, BANK], U32, name="w_codes%d_%d" % (g, rh), align_bytes=64)
                w_scale[g, rh] = keep.tile([P, BANK], U8, name="w_scale%d_%d" % (g, rh), align_bytes=64)

        nc.vector.memset(vec_rows[:], 0.0)
        nc.vector.memset(cs_raw[:].rearrange("p a n -> p (a n)").bitcast(I32), 0)
        make_identity(nc, ident16[:])
        make_identity(nc, ident32[:])

        def load_x(j):
            nc.sync.dma_start(out=x_raw[j][:], in_=x_rows[:, j, :])

        def load_w(g):
            for t in range(SLOTS):
                nc.sync.dma_start(out=w_raw[g][:, t, :], in_=w_sets[SLOTS * g + t])

        nc.sync.dma_start(out=xn_cols[:], in_=xn.rearrange("(p j) -> p j", j=ROW_TILES))
        load_x(0)
        for row0, vec in ((0, cn), (16, stiff)):
            nc.sync.dma_start(
                out=vec_rows[row0 : row0 + 16, :].rearrange("c (q r) -> c q r", r=8),
                in_=vec.rearrange("(q c r) -> c q r", q=16, c=16, r=8),
            )
        for j in (1, 2, 3):
            load_x(j)
        for quad in range(4):
            nc.sync.dma_start(
                out=cs_raw[32 * quad : 32 * quad + 4, :, :].bitcast(I32),
                in_=c_scales[:, 4 * quad : 4 * quad + 4, :].rearrange("a r n -> r a n").bitcast(I32),
            )
        nc.sync.dma_start(out=c_raw[:].bitcast(I32), in_=c_words.rearrange("a p n -> p a n").bitcast(I32))
        load_w(0)
        for j in (4, 5, 6, 7):
            load_x(j)
        load_w(1)
        load_w(2)
        load_w(3)

        x_banks = {}
        x_pairs = {}

        x_sorted = {}

        def sort_x(j):
            x_sorted[j] = ring.tile([P, K // 2], F32, name="x_sorted", bufs=4)
            nc.vector.tensor_copy(
                out=x_sorted[j][:].rearrange("p (a u w) -> p a u w", a=K_PASSES, u=2),
                in_=x_raw[j][:].bitcast(F32).rearrange("p (a w u) -> p a u w", a=K_PASSES, u=2),
            )

        def turn_x(j):
            bank = ps_b.tile([P, BANK], F32, name="bank_b")
            words = x_raw[j][:].bitcast(F32)
            for kp in range(K_PASSES):
                for u in range(2):
                    col0 = (2 * kp + u) * P
                    if j in x_sorted:
                        block = x_sorted[j][:, col0 : col0 + P]
                    else:
                        block = words[:, 256 * kp + u : 256 * (kp + 1) : 2]
                    nc.tensor.transpose(bank[:, col0 : col0 + P], block, ident32[:])
            x_banks[j] = bank

        def spill_x(j, on_vector):
            if j % 2 == 0:
                x_pairs[j // 2] = ring.tile([P, K_PASSES, 2 * P, 2], F32, name="x_pair", align_bytes=64)
            dst = x_pairs[j // 2][:, :, (j % 2) * P : (j % 2 + 1) * P, :]
            src = x_banks[j][:].rearrange("p (a u m) -> p a m u", a=K_PASSES, u=2)
            if on_vector:
                nc.vector.tensor_copy(out=dst, in_=src)
            else:
                nc.scalar.copy(out=dst, in_=src)

        def quantise_x(a):
            h, col0 = a // 2, (a % 2) * 2 * P
            for kp in range(K_PASSES):
                nc.vector.quantize_mx(
                    out=x_codes[h][:, kp, col0 : col0 + 2 * P].bitcast(E4M3),
                    scales=x_scale[h][:, kp, col0 : col0 + 2 * P],
                    in_=x_pairs[a][:, kp, :, :].rearrange("p m u -> p (m u)").bitcast(BF16),
                )

        def deal_c(g):
            src = c_raw[:].bitcast(I32).rearrange("p a (q c e) -> p a c q e", q=16, c=16)
            nc.vector.tensor_copy(
                out=c_codes[g][:].bitcast(I32).rearrange("p a (c q e) -> p a c q e", c=SLOTS, q=16),
                in_=src[:, :, SLOTS * g : SLOTS * (g + 1), :, :],
            )

        def deal_cs(g):
            src = cs_raw[:].bitcast(I32).rearrange("p a (q c e) -> p a c q e", q=16, c=16)
            nc.vector.tensor_copy(
                out=c_scale[g][:].bitcast(I32).rearrange("p a (c q e) -> p a c q e", c=SLOTS, q=16),
                in_=src[:, :, SLOTS * g : SLOTS * (g + 1), :, :],
            )

        w_mixed = {}

        def mix_w(g, rh, part):
            mixed = ring.tile([P, W_PART, SLOTS], BF16, name="w_mixed", bufs=6, align_bytes=64)
            col0 = rh * BANK + part * W_PART
            nc.scalar.copy(
                out=mixed[:].rearrange("p (c i) t -> p c t i", i=4),
                in_=w_raw[g][:, :, col0 : col0 + W_PART].rearrange("p t (c i) -> p c t i", i=4),
            )
            w_mixed[g, rh, part] = mixed

        def quantise_w(g, rh, part):
            cols = slice(part * W_PART, (part + 1) * W_PART)
            nc.vector.quantize_mx(
                out=w_codes[g, rh][:, cols].bitcast(E4M3),
                scales=w_scale[g, rh][:, cols],
                in_=w_mixed[g, rh, part][:].rearrange("p f t -> p (f t)"),
            )

        cross = {}

        def cross_mm(step, t):
            h, g = divmod(step, N_PASSES)
            bank = ps_a.tile([P, BANK], F32, name="bank_a")
            for kp in range(K_PASSES):
                nc.tensor.matmul_mx(
                    out=bank[:],
                    lhsT=c_codes[g][:, kp, 2 * P * t : 2 * P * (t + 1)].bitcast(E2M1),
                    lhsT_scale=c_scale[g][:, kp, P * t : P * (t + 1)],
                    rhs=x_codes[h][:, kp, :].bitcast(E4M3),
                    rhs_scale=x_scale[h][:, kp, :],
                    start=(kp == 0),
                    stop=(kp == K_PASSES - 1),
                )
            cross[step, t] = bank

        scaled = {}
        logs = {}

        def add_norms(step, t):
            h, g = divmod(step, N_PASSES)
            if t == 0:
                scaled[step] = ring.tile([P, SLOTS, BANK], F32, name="scaled", bufs=3)
            c = SLOTS * g + t
            nc.vector.scalar_tensor_tensor(
                out=scaled[step][:, t, :],
                in0=xn_wide[:, h * BANK : (h + 1) * BANK],
                scalar=vec_cols[:, c : c + 1],
                in1=cross[step, t][:],
                op0=ALU.add,
                op1=ALU.add,
            )

        def clamp_scale(step, t):
            c = SLOTS * (step % N_PASSES) + t
            nc.vector.tensor_scalar(
                out=scaled[step][:, t, :],
                in0=scaled[step][:, t, :],
                scalar1=1.0,
                scalar2=vec_cols[:, 16 + c : 17 + c],
                op0=ALU.max,
                op1=ALU.mult,
            )

        def take_log(step, t):
            c = SLOTS * (step % N_PASSES) + t
            if t == 0:
                logs[step] = ring.tile([P, SLOTS, BANK], F32, name="logs")
            nc.scalar.activation(
                out=logs[step][:, t, :],
                in_=scaled[step][:, t, :],
                func=ACT.Ln,
                scale=inverse[:, c : c + 1],
                bias=residual[:, c : c + 1],
            )

        u_mixed = {}
        u_codes = {}
        u_scale = {}

        def multiply(step, col0, col1, engine):
            if step not in u_mixed:
                u_mixed[step] = ring.tile(
                    [P, BANK, SLOTS], BF16, name="u_last" if step == STEPS - 1 else "u_mixed", bufs=1, align_bytes=64
                )
            cols = slice(col0, col1)
            engine.tensor_tensor(
                out=u_mixed[step][:, cols, :].rearrange("p (c i) t -> p c t i", i=2),
                in0=scaled[step][:, :, cols].rearrange("p t (c i) -> p c t i", i=2),
                in1=logs[step][:, :, cols].rearrange("p t (c i) -> p c t i", i=2),
                op=ALU.mult,
            )

        def quantise_u(step, col0, width):
            codes = keep.tile([P, width], U32, name="u_codes%d_%d" % (step, col0), align_bytes=64)
            scales = keep.tile([P, width], U8, name="u_scale%d_%d" % (step, col0), align_bytes=64)
            nc.vector.quantize_mx(
                out=codes[:].bitcast(E5M2),
                scales=scales[:],
                in_=u_mixed[step][:, col0 : col0 + width, :].rearrange("p m t -> p (m t)"),
            )
            for j in range(width // P):
                u_codes[step, col0 // P + j] = codes[:, j * P : (j + 1) * P]
                u_scale[step, col0 // P + j] = scales[:, j * P : (j + 1) * P]

        sums = {}

        def out_mm(h, j, rh, g, pool):
            if g == 0:
                sums[h, j, rh] = pool.tile([P, BANK], F32, name="bank_a" if pool is ps_a else "bank_b")
            nc.tensor.matmul_mx(
                out=sums[h, j, rh][:],
                lhsT=u_codes[N_PASSES * h + g, j].bitcast(E5M2),
                lhsT_scale=u_scale[N_PASSES * h + g, j],
                rhs=w_codes[g, rh][:].bitcast(E4M3),
                rhs_scale=w_scale[g, rh][:],
                start=(g == 0),
                stop=(g == N_PASSES - 1),
            )

        def out_passes(h, rh, passes, pool):
            for j in range(TILES_PER_HALF):
                for g in passes:
                    out_mm(h, j, rh, g, pool)

        def store(h, j, rh, on_vector):
            result = ring.tile([P, BANK], F32, name="result", bufs=6)
            if on_vector:
                nc.vector.tensor_copy(out=result[:], in_=sums[h, j, rh][:])
            else:
                nc.scalar.copy(out=result[:], in_=sums[h, j, rh][:])
            nc.sync.dma_start(out=out_rows[:, TILES_PER_HALF * h + j, rh * BANK : (rh + 1) * BANK], in_=result[:])

        xn_bank = ps_a.tile([P, M], BF16, name="bank_a")
        for j in range(ROW_TILES):
            nc.tensor.transpose(xn_bank[:, j * P : (j + 1) * P], xn_cols[:, j : j + 1].to_broadcast([P, P]), ident16[:])
        vec_bank = ps_a.tile([P, P], BF16, name="bank_a")
        nc.tensor.transpose(vec_bank[:], vec_rows[:], ident16[:])
        for j in range(TILES_PER_HALF):
            sort_x(j)
            turn_x(j)
            if j == 0:
                nc.scalar.copy(out=xn_wide[:], in_=xn_bank[:])
            if j == 1:
                nc.vector.tensor_copy(out=vec_cols[:], in_=vec_bank[:, 0:32])
            spill_x(j, False)
        stiff_cols = vec_cols[:, 16:32]
        nc.vector.scalar_tensor_tensor(out=divisor[:], in0=stiff_cols, scalar=0.0, in1=stiff_cols, op0=ALU.is_equal, op1=ALU.add)
        nc.vector.tensor_scalar(out=neg_stiff[:], in0=stiff_cols, scalar1=-1.0, scalar2=None, op0=ALU.mult)
        quantise_x(0)
        nc.vector.reciprocal(out=inverse[:], in_=divisor[:])
        deal_cs(0)
        quantise_x(1)
        deal_c(0)
        for c in range(16):
            nc.scalar.activation(
                out=residual[:, c : c + 1], in_=neg_stiff[:, c : c + 1], func=ACT.Identity, scale=inverse[:, c : c + 1], bias=1.0
            )
        for t in range(SLOTS):
            cross_mm(0, t)
        for g in range(1, N_PASSES):
            deal_cs(g)
            deal_c(g)

        w_order = [(g, rh, part) for rh in range(R_HALVES) for g in range(N_PASSES) for part in range(BANK // W_PART)]
        mixes = {-1: w_order[0:2], 0: w_order[2:5], 1: w_order[5:8], 2: w_order[8:12], 3: w_order[12:15], 4: w_order[15:16]}
        for key in mixes[-1]:
            mix_w(*key)

        last = STEPS - 1
        for step in range(STEPS):
            share = P
            if step >= 1:
                multiply(step - 1, 0, share, nc.gpsimd)
            if step in (5, 6):
                out_passes(0, step - 5, [3] if step == 5 else [2, 3], ps_b)
                for j in range(TILES_PER_HALF):
                    store(0, j, step - 5, False)
            for t in range(SLOTS):
                add_norms(step, t)
                if step + 1 < STEPS:
                    cross_mm(step + 1, t)
                if step == 0 and t >= 1:
                    clamp_scale(step, t - 1)
                    take_log(step, t - 1)
            if step in (0, 1):
                turn_x(4 + 2 * step)
                turn_x(5 + 2 * step)
            if step in (2, 3, 4):
                out_passes(0, 0, [step - 2], ps_b)
            if step == 5:
                out_passes(0, 1, [0, 1], ps_b)
            if step == 6:
                out_passes(1, 0, [0], ps_b)
            if step == 7:
                out_passes(1, 0, [1], ps_b)
                out_passes(1, 1, [0, 1], ps_a)
            for t in range(SLOTS - 1 if step == 0 else 0, SLOTS):
                if t == SLOTS - 1 and 1 <= step < last:
                    multiply(step - 1, share, BANK, nc.vector)
                clamp_scale(step, t)
                take_log(step, t)
            if step in (1, 2):
                quantise_x(step + 1)
            for key in mixes.get(step - 1, []):
                quantise_w(*key)
            if step in (0, 1):
                spill_x(4 + 2 * step, False)
                spill_x(5 + 2 * step, False)
            for key in mixes.get(step, []):
                mix_w(*key)
            if 1 <= step < last:
                quantise_u(step - 1, 0, BANK)

        def finish(step, j):
            quantise_u(step, j * P, P)
            out_mm(1, j, 0, step - N_PASSES, ps_b)
            out_mm(1, j, 1, step - N_PASSES, ps_a)

        def multiply_tile(step, j):
            multiply(step, j * P, (j + 1) * P, nc.vector)

        multiply_tile(last - 1, 1)
        finish(last - 1, 0)
        multiply_tile(last - 1, 2)
        finish(last - 1, 1)
        multiply_tile(last, 0)
        finish(last - 1, 2)
        finish(last, 0)
        store(1, 0, 0, False)
        store(1, 0, 1, False)
        multiply_tile(last, 1)
        multiply_tile(last - 1, 3)
        finish(last, 1)
        store(1, 1, 0, False)
        store(1, 1, 1, False)
        multiply_tile(last, 2)
        finish(last - 1, 3)
        finish(last, 2)
        store(1, 2, 0, False)
        store(1, 2, 1, False)
        multiply_tile(last, 3)
        finish(last, 3)
        store(1, 3, 0, False)
        store(1, 3, 1, True)
